import numpy as np, ml_dtypes
CORES = [6,14,22,30,38,134,142,150,158]
N = 9
V, K = 512, 2
T = V * K; R = V
CAPP = 256
def entries(a): return a.T.reshape(-1)
def pack(v, P): return np.ascontiguousarray(np.asarray(v, np.int32).reshape(-1, P).T)
def lists(rng, how):
    I = rng.integers(0, N * R, (N, T))
    O = np.stack([rng.permutation(np.repeat(np.arange(N), CAPP))[:T] for r in range(N)])
    if how == "full": O = np.stack([rng.permutation(np.repeat(rng.permutation(N)[:T // CAPP], CAPP)) for r in range(N)])
    I = R * O + rng.integers(0, R, (N, T))
    if how == "alike": I = R * O + rng.integers(0, R, (N, 1))
    if how == "edge": I = R * O + np.where(rng.random((N, T)) < 0.5, 0, R - 1)
    if how == "sorted": I = np.sort(I, axis=1)
    return {"nb": np.stack([pack(I[r], 16) for r in range(N)])}
def setup_inputs(rng):
    w = (rng.standard_normal((128, 128), dtype=np.float32) / 16).astype(ml_dtypes.bfloat16)
    return dict({"x": rng.standard_normal((N, 128, V), dtype=np.float32).astype(ml_dtypes.bfloat16), "w": np.broadcast_to(w, (N, 128, 128)).copy()}, **lists(rng, "uniform"))
def setup_inputs_alike(rng):
    d = setup_inputs(rng); d.update(lists(rng, "alike"))
    for k in ("x",): d[k] = (d[k].astype(np.float32) * 1024.0).astype(d[k].dtype)
    return d
def setup_inputs_edge(rng):
    d = setup_inputs(rng); d.update(lists(rng, "edge"))
    for k in ("x",): d[k] = (d[k].astype(np.float32) * (1 / 1024.0)).astype(d[k].dtype)
    return d
def setup_inputs_full(rng):
    d = setup_inputs(rng); d.update(lists(rng, "full"))
    return d
def setup_inputs_sorted(rng):
    d = setup_inputs(rng); d.update(lists(rng, "sorted"))
    return d
def check_inputs(x):
    bad = []
    if x["nb"].min() < 0 or x["nb"].max() >= N * V: bad.append("nb out of range")
    if max(int(np.bincount(entries(a) // V, minlength=N).max()) for a in x["nb"]) > CAPP: bad.append("more than CAPP entries of a list point into one rank's part")
    if not all(np.array_equal(a, x["w"][0]) for a in x["w"]): bad.append("w isn't alike on all ranks")
    return bad
def reference(x, w, nb):
    X, W = x.astype(np.float64), w.astype(np.float64)
    A = np.concatenate(list(X), axis=1)
    return {"y": np.stack([np.maximum(W[r].T @ (X[r] + A[:, entries(nb[r])].reshape(128, V, K).sum(axis=2)), 0.0) for r in range(N)]).astype(ml_dtypes.bfloat16)}

@@ -1,0 +1,178 @@
+from concourse.bass import DstId, RemoteDMATransfer
+from concourse.mybir import AluOpType, ActivationFunctionType
+
+N, V = 9, 512
+WORLD = 256
+CH = 128
+NCH = V // CH
+
+SCRATCH = {
+    "win": ("sbuf", [128, N * V], "bfloat16"),
+    "wsb": ("sbuf", [128, 128], "bfloat16"),
+    "idx": ("sbuf", [128, 64], "int32"),
+    "off": ("sbuf", [128, 64], "uint16"),
+    "gat": ("sbuf", [128, 2 * V], "bfloat16"),
+    "ysb": ("sbuf", [128, V], "bfloat16"),
+    "ps0": ("psum", [128, 512], "float32"),
+    "ps1": ("psum", [128, 512], "float32"),
+    "ps2": ("psum", [128, 512], "float32"),
+    "ps3": ("psum", [128, 512], "float32"),
+}
+SEMAPHORES = ["sx", "sw", "snb", "soff", "fed", "arr", "sent", "sy",
+              "g0", "g1", "g2", "g3", "m0", "m1", "m2", "m3", "r0", "r1", "r2", "r3"]
+
+_CACHE = {}
+
+
+def _chip(topo, c):
+    return (topo.host(c), topo.chip(c))
+
+
+def _route(topo, src, dst):
+    d = topo.die(src)
+    if topo.same_plane(src, dst):
+        return [("out", _chip(topo, src), d), ("in", _chip(topo, dst), d)]
+    if topo.mates(src, dst):
+        return [("mate", _chip(topo, src), d)]
+    m = [q for q in range(WORLD) if topo.mates(src, q)][0]
+    return [("mate", _chip(topo, src), d), ("out", _chip(topo, m), d), ("in", _chip(topo, dst), d)]
+
+
+def _count(m):
+    return len([b for b in range(16) if (m >> b) & 1])
+
+
+def plan(topo, cores):
+    if "plan" in _CACHE:
+        return _CACHE["plan"]
+    n = len(cores)
+    same, other = [], []
+    for c in cores:
+        port = [h for h in range(WORLD) if h != c and _chip(topo, h) == _chip(topo, c)
+                and all(topo.may_write(h, d) for d in cores if d != h)]
+        same.append([h for h in port if topo.die(h) == topo.die(c)])
+        other.append([h for h in port if topo.die(h) != topo.die(c)])
+    routes = [[[None if i == j else _route(topo, s, cores[j]) for s in (cores[i], other[i][0])]
+               for j in range(n)] for i in range(n)]
+    far = [[((j - i) % n - 1) // 2 % 2 if i != j else 0 for j in range(n)] for i in range(n)]
+
+    def score():
+        load = {}
+        for i in range(n):
+            for j in range(n):
+                if i != j:
+                    for l in routes[i][j][far[i][j]]:
+                        load[l] = load.get(l, 0) + 1
+        return sum(v * v for v in load.values())
+
+    best, moved = score(), True
+    while moved:
+        moved = False
+        for i in range(n):
+            for a in range(n):
+                for b in range(n):
+                    if a != i and b != i and far[i][a] == 1 and far[i][b] == 0:
+                        far[i][a], far[i][b] = 0, 1
+                        s = score()
+                        if s < best:
+                            best, moved = s, True
+                        else:
+                            far[i][a], far[i][b] = 1, 0
+    out = []
+    for i in range(n):
+        c = cores[i]
+        f = [j for j in range(n) if j != i and far[i][j] == 1]
+        k = [j for j in range(n) if j != i and far[i][j] == 0]
+        lo = topo.mask(c, same[i][0])
+        for h in (c, same[i][0], other[i][0], other[i][1]):
+            for j in range(n):
+                if j != i:
+                    lo &= topo.mask(h, cores[j])
+        hi = topo.mask(c, same[i][0]) & topo.mask(c, other[i][0]) & topo.mask(c, other[i][1]) & ~lo
+        out.append([(other[i][0], f[0:2], lo, lo), (other[i][1], f[2:4], lo, hi), (c, k[0:3], lo, 0), (same[i][0], k[3:4], lo, hi)])
+    _CACHE["plan"] = out
+    return out
+
+
+def _send(T, topo, core, slot, dsts, mask, sem):
+    ids = []
+    for d in dsts:
+        rid, pid = topo.addr(d, core)
+        ids.append(DstId(rid=rid, pnc=pid))
+    ap = T.win[:, slot * V:(slot + 1) * V]
+    return RemoteDMATransfer(dst_ids=ids, dma_engine_mask=mask, remote_sem=sem, srcs=[ap], dsts=[ap for d in dsts], alu_op=0)
+
+
+def rank_program(g, core, T, topo):
+    cores = list(T.cores)
+    P = plan(topo, cores)
+    rank = T.rank_of(core)
+    S = T.sem
+    if rank is None:
+        for i in range(N):
+            for h, dst, m, fm in P[i]:
+                if h == core:
+                    g.wait_ge(S.fed, _count(fm))
+                    g.remote_dma_fused([_send(T, topo, core, i, [cores[j] for j in dst], m, S.arr)], local_sem=S.sent)
+                    g.wait_ge(S.sent, _count(m))
+        return
+
+    fa, fb, me, nr = P[rank]
+    own = T.win[:, rank * V:(rank + 1) * V]
+    g.sync.dma_start(own, T.x[:, :]).then_inc(S.sx, 16)
+    g.scalar.dma_start(T.wsb[:, :], T.w[:, :]).then_inc(S.sw, 16)
+    for q in range(8):
+        (g.sync if q % 2 else g.scalar).dma_start(T.idx[16 * q:16 * q + 16, :], T.nb[:, :]).then_inc(S.snb, 16)
+
+    g.wait_ge(S.sx, 16)
+    g.remote_dma_fused([_send(T, topo, core, rank, [fa[0]], fa[3], S.fed),
+                        _send(T, topo, core, rank, [fb[0]], fb[3], S.fed)], local_sem=S.sent)
+    g.remote_dma_fused([_send(T, topo, core, rank, [cores[j] for j in me[1]], me[2], S.arr),
+                        _send(T, topo, core, rank, [nr[0]], nr[3], S.fed)], local_sem=S.sent)
+
+    landed = sum(_count(m) for i in range(N) for h, dst, m, fm in P[i] if rank in dst)
+
+    ps = [T.ps0, T.ps1, T.ps2, T.ps3]
+    gs = [S.g0, S.g1, S.g2, S.g3]
+    ms = [S.m0, S.m1, S.m2, S.m3]
+    rs = [S.r0, S.r1, S.r2, S.r3]
+    v, s, t = g.vector, g.scalar, g.tensor
+
+    v.wait_ge(S.snb, 128)
+    v.tensor_copy(T.off[:, :], T.idx[:, :]).then_inc(S.soff, 1)
+
+    t.wait_ge(S.sx, 16)
+    t.wait_ge(S.sw, 16)
+    for k in range(NCH):
+        t.matmul(ps[k][:, 0:CH], T.wsb[:, :], T.win[:, rank * V + k * CH:rank * V + (k + 1) * CH], True, False)
+
+    for e in (v, s):
+        e.wait_ge(S.soff, 1)
+        e.wait_ge(S.sx, 16)
+        e.wait_ge(S.arr, landed)
+    oc = 2 * CH // 16
+    for k in range(NCH):
+        src = T.win[:, 0:N * V].indirect(T.off[:, k * oc:(k + 1) * oc])
+        dst = T.gat[:, k * 2 * CH:(k + 1) * 2 * CH]
+        if k % 2 == 0:
+            v.tensor_copy(dst, src).then_inc(gs[k], 1)
+        else:
+            s.activation(dst, src, ActivationFunctionType.Copy).then_inc(gs[k], 1)
+    for k in range(NCH):
+        t.wait_ge(gs[k], 1)
+        t.matmul(ps[k][:, 0:CH], T.wsb[:, :], T.gat[:, k * 2 * CH:(k + 1) * 2 * CH:2], False, False)
+        t.matmul(ps[k][:, 0:CH], T.wsb[:, :], T.gat[:, k * 2 * CH + 1:(k + 1) * 2 * CH:2], False, True).then_inc(ms[k], 1)
+    for k in range(NCH):
+        dst = T.ysb[:, k * CH:(k + 1) * CH]
+        if k % 2 == 0:
+            v.wait_ge(ms[k], 1)
+            v.tensor_scalar(dst, ps[k][:, 0:CH], 0.0, None, AluOpType.max).then_inc(rs[k], 1)
+        else:
+            s.wait_ge(ms[k], 1)
+            s.activation(dst, ps[k][:, 0:CH], ActivationFunctionType.Relu).then_inc(rs[k], 1)
+    for a in range(NCH // 2):
+        g.sync.wait_ge(rs[2 * a], 1)
+        g.sync.wait_ge(rs[2 * a + 1], 1)
+        g.sync.dma_start(T.y[:, 2 * a * CH:(2 * a + 2) * CH], T.ysb[:, 2 * a * CH:(2 * a + 2) * CH]).then_inc(S.sy, 16)
+    g.sync.wait_ge(S.sy, 16 * (NCH // 2))
+    g.wait_ge(S.sent, _count(fa[3]) + _count(fb[3]) + _count(me[2]) + _count(nr[3]))

@@ -5,6 +5,9 @@ N, V = 9, 512
 WORLD = 256
 CH = 128
 NCH = V // CH
+FAR, NEAR = [2, 1], [2]
+CALLS = [[("far", 0, "lo"), ("near", 0, "hi")], [("own", 0, "lo"), ("far", 1, "hi")]]
+HSEND = "lo"
 
 SCRATCH = {
     "win": ("sbuf", [128, N * V], "bfloat16"),
@@ -54,7 +57,9 @@ def plan(topo, cores):
         other.append([h for h in port if topo.die(h) != topo.die(c)])
     routes = [[[None if i == j else _route(topo, s, cores[j]) for s in (cores[i], other[i][0])]
                for j in range(n)] for i in range(n)]
-    far = [[((j - i) % n - 1) // 2 % 2 if i != j else 0 for j in range(n)] for i in range(n)]
+    nf = sum(FAR)
+    pick = sorted(range(1, n), key=lambda o: (1 - (o - 1) // 2 % 2, o))[0:nf]
+    far = [[1 if (j - i) % n in pick else 0 for j in range(n)] for i in range(n)]
 
     def score():
         load = {}
@@ -79,17 +84,45 @@ def plan(topo, cores):
                         else:
                             far[i][a], far[i][b] = 1, 0
     out = []
+    late = [0 for j in range(n)]
     for i in range(n):
         c = cores[i]
         f = [j for j in range(n) if j != i and far[i][j] == 1]
-        k = [j for j in range(n) if j != i and far[i][j] == 0]
+        k = sorted([j for j in range(n) if j != i and far[i][j] == 0], key=lambda j: (late[j], (j - i) % n))
+        for j in k[0:sum(NEAR)]:
+            late[j] += 1
         lo = topo.mask(c, same[i][0])
         for h in (c, same[i][0], other[i][0], other[i][1]):
             for j in range(n):
                 if j != i:
                     lo &= topo.mask(h, cores[j])
         hi = topo.mask(c, same[i][0]) & topo.mask(c, other[i][0]) & topo.mask(c, other[i][1]) & ~lo
-        out.append([(other[i][0], f[0:2], lo, lo), (other[i][1], f[2:4], lo, hi), (c, k[0:3], lo, 0), (same[i][0], k[3:4], lo, hi)])
+        masks = {"lo": lo, "hi": hi, "all": lo | hi}
+        for nm in ("lo", "hi"):
+            bs = [b for b in range(16) if (masks[nm] >> b) & 1]
+            masks[nm + "0"] = sum(1 << b for b in bs[0:len(bs) // 2])
+            masks[nm + "1"] = sum(1 << b for b in bs[len(bs) // 2:])
+        who, pos = {}, 0
+        for a, ld in enumerate(FAR):
+            who[("far", a)] = (other[i][a], f[pos:pos + ld])
+            pos += ld
+        pos = 0
+        for a, ld in enumerate(NEAR):
+            who[("near", a)] = (same[i][a], k[pos:pos + ld])
+            pos += ld
+        who[("own", 0)] = (c, k[pos:])
+        senders, calls = [], []
+        for call in CALLS:
+            calls.append([])
+            for what, a, nm in call:
+                h, dst = who[(what, a)]
+                if what == "own":
+                    senders.append((h, dst, masks[nm], 0))
+                    calls[-1].append(([cores[j] for j in dst], masks[nm], "arr"))
+                else:
+                    senders.append((h, dst, masks[HSEND], masks[nm]))
+                    calls[-1].append(([h], masks[nm], "fed"))
+        out.append((senders, calls))
     _CACHE["plan"] = out
     return out
 
@@ -110,14 +143,13 @@ def rank_program(g, core, T, topo):
     S = T.sem
     if rank is None:
         for i in range(N):
-            for h, dst, m, fm in P[i]:
+            for h, dst, m, fm in P[i][0]:
                 if h == core:
                     g.wait_ge(S.fed, _count(fm))
                     g.remote_dma_fused([_send(T, topo, core, i, [cores[j] for j in dst], m, S.arr)], local_sem=S.sent)
                     g.wait_ge(S.sent, _count(m))
         return
 
-    fa, fb, me, nr = P[rank]
     own = T.win[:, rank * V:(rank + 1) * V]
     g.sync.dma_start(own, T.x[:, :]).then_inc(S.sx, 16)
     g.scalar.dma_start(T.wsb[:, :], T.w[:, :]).then_inc(S.sw, 16)
@@ -125,12 +157,12 @@ def rank_program(g, core, T, topo):
         (g.sync if q % 2 else g.scalar).dma_start(T.idx[16 * q:16 * q + 16, :], T.nb[:, :]).then_inc(S.snb, 16)
 
     g.wait_ge(S.sx, 16)
-    g.remote_dma_fused([_send(T, topo, core, rank, [fa[0]], fa[3], S.fed),
-                        _send(T, topo, core, rank, [fb[0]], fb[3], S.fed)], local_sem=S.sent)
-    g.remote_dma_fused([_send(T, topo, core, rank, [cores[j] for j in me[1]], me[2], S.arr),
-                        _send(T, topo, core, rank, [nr[0]], nr[3], S.fed)], local_sem=S.sent)
+    left = 0
+    for call in P[rank][1]:
+        g.remote_dma_fused([_send(T, topo, core, rank, dsts, m, S[nm]) for dsts, m, nm in call], local_sem=S.sent)
+        left += sum(_count(m) for dsts, m, nm in call)
 
-    landed = sum(_count(m) for i in range(N) for h, dst, m, fm in P[i] if rank in dst)
+    landed = sum(_count(m) for i in range(N) for h, dst, m, fm in P[i][0] if rank in dst)
 
     ps = [T.ps0, T.ps1, T.ps2, T.ps3]
     gs = [S.g0, S.g1, S.g2, S.g3]
@@ -175,4 +207,4 @@ def rank_program(g, core, T, topo):
         g.sync.wait_ge(rs[2 * a + 1], 1)
         g.sync.dma_start(T.y[:, 2 * a * CH:(2 * a + 2) * CH], T.ysb[:, 2 * a * CH:(2 * a + 2) * CH]).then_inc(S.sy, 16)
     g.sync.wait_ge(S.sy, 16 * (NCH // 2))
-    g.wait_ge(S.sent, _count(fa[3]) + _count(fb[3]) + _count(me[2]) + _count(nr[3]))
+    g.wait_ge(S.sent, left)

from concourse.bass import DstId, RemoteDMATransfer
from concourse.mybir import AluOpType, ActivationFunctionType

N, V = 9, 512
WORLD = 256
CH = 128
NCH = V // CH
FAR, NEAR = [2, 1], [2]
CALLS = [[("far", 0, "lo"), ("near", 0, "hi")], [("own", 0, "lo"), ("far", 1, "hi")]]
HSEND = "lo"

SCRATCH = {
    "win": ("sbuf", [128, N * V], "bfloat16"),
    "wsb": ("sbuf", [128, 128], "bfloat16"),
    "idx": ("sbuf", [128, 64], "int32"),
    "off": ("sbuf", [128, 64], "uint16"),
    "gat": ("sbuf", [128, 2 * V], "bfloat16"),
    "ysb": ("sbuf", [128, V], "bfloat16"),
    "ps0": ("psum", [128, 512], "float32"),
    "ps1": ("psum", [128, 512], "float32"),
    "ps2": ("psum", [128, 512], "float32"),
    "ps3": ("psum", [128, 512], "float32"),
}
SEMAPHORES = ["sx", "sw", "snb", "soff", "fed", "arr", "sent", "sy",
              "g0", "g1", "g2", "g3", "m0", "m1", "m2", "m3", "r0", "r1", "r2", "r3"]

_CACHE = {}


def _chip(topo, c):
    return (topo.host(c), topo.chip(c))


def _route(topo, src, dst):
    d = topo.die(src)
    if topo.same_plane(src, dst):
        return [("out", _chip(topo, src), d), ("in", _chip(topo, dst), d)]
    if topo.mates(src, dst):
        return [("mate", _chip(topo, src), d)]
    m = [q for q in range(WORLD) if topo.mates(src, q)][0]
    return [("mate", _chip(topo, src), d), ("out", _chip(topo, m), d), ("in", _chip(topo, dst), d)]


def _count(m):
    return len([b for b in range(16) if (m >> b) & 1])


def plan(topo, cores):
    if "plan" in _CACHE:
        return _CACHE["plan"]
    n = len(cores)
    same, other = [], []
    for c in cores:
        port = [h for h in range(WORLD) if h != c and _chip(topo, h) == _chip(topo, c)
                and all(topo.may_write(h, d) for d in cores if d != h)]
        same.append([h for h in port if topo.die(h) == topo.die(c)])
        other.append([h for h in port if topo.die(h) != topo.die(c)])
    routes = [[[None if i == j else _route(topo, s, cores[j]) for s in (cores[i], other[i][0])]
               for j in range(n)] for i in range(n)]
    nf = sum(FAR)
    pick = sorted(range(1, n), key=lambda o: (1 - (o - 1) // 2 % 2, o))[0:nf]
    far = [[1 if (j - i) % n in pick else 0 for j in range(n)] for i in range(n)]

    def score():
        load = {}
        for i in range(n):
            for j in range(n):
                if i != j:
                    for l in routes[i][j][far[i][j]]:
                        load[l] = load.get(l, 0) + 1
        return sum(v * v for v in load.values())

    best, moved = score(), True
    while moved:
        moved = False
        for i in range(n):
            for a in range(n):
                for b in range(n):
                    if a != i and b != i and far[i][a] == 1 and far[i][b] == 0:
                        far[i][a], far[i][b] = 0, 1
                        s = score()
                        if s < best:
                            best, moved = s, True
                        else:
                            far[i][a], far[i][b] = 1, 0
    out = []
    late = [0 for j in range(n)]
    for i in range(n):
        c = cores[i]
        f = [j for j in range(n) if j != i and far[i][j] == 1]
        k = sorted([j for j in range(n) if j != i and far[i][j] == 0], key=lambda j: (late[j], (j - i) % n))
        for j in k[0:sum(NEAR)]:
            late[j] += 1
        lo = topo.mask(c, same[i][0])
        for h in (c, same[i][0], other[i][0], other[i][1]):
            for j in range(n):
                if j != i:
                    lo &= topo.mask(h, cores[j])
        hi = topo.mask(c, same[i][0]) & topo.mask(c, other[i][0]) & topo.mask(c, other[i][1]) & ~lo
        masks = {"lo": lo, "hi": hi, "all": lo | hi}
        for nm in ("lo", "hi"):
            bs = [b for b in range(16) if (masks[nm] >> b) & 1]
            masks[nm + "0"] = sum(1 << b for b in bs[0:len(bs) // 2])
            masks[nm + "1"] = sum(1 << b for b in bs[len(bs) // 2:])
        who, pos = {}, 0
        for a, ld in enumerate(FAR):
            who[("far", a)] = (other[i][a], f[pos:pos + ld])
            pos += ld
        pos = 0
        for a, ld in enumerate(NEAR):
            who[("near", a)] = (same[i][a], k[pos:pos + ld])
            pos += ld
        who[("own", 0)] = (c, k[pos:])
        senders, calls = [], []
        for call in CALLS:
            calls.append([])
            for what, a, nm in call:
                h, dst = who[(what, a)]
                if what == "own":
                    senders.append((h, dst, masks[nm], 0))
                    calls[-1].append(([cores[j] for j in dst], masks[nm], "arr"))
                else:
                    senders.append((h, dst, masks[HSEND], masks[nm]))
                    calls[-1].append(([h], masks[nm], "fed"))
        out.append((senders, calls))
    _CACHE["plan"] = out
    return out


def _send(T, topo, core, slot, dsts, mask, sem):
    ids = []
    for d in dsts:
        rid, pid = topo.addr(d, core)
        ids.append(DstId(rid=rid, pnc=pid))
    ap = T.win[:, slot * V:(slot + 1) * V]
    return RemoteDMATransfer(dst_ids=ids, dma_engine_mask=mask, remote_sem=sem, srcs=[ap], dsts=[ap for d in dsts], alu_op=0)


def rank_program(g, core, T, topo):
    cores = list(T.cores)
    P = plan(topo, cores)
    rank = T.rank_of(core)
    S = T.sem
    if rank is None:
        for i in range(N):
            for h, dst, m, fm in P[i][0]:
                if h == core:
                    g.wait_ge(S.fed, _count(fm))
                    g.remote_dma_fused([_send(T, topo, core, i, [cores[j] for j in dst], m, S.arr)], local_sem=S.sent)
                    g.wait_ge(S.sent, _count(m))
        return

    own = T.win[:, rank * V:(rank + 1) * V]
    g.sync.dma_start(own, T.x[:, :]).then_inc(S.sx, 16)
    g.scalar.dma_start(T.wsb[:, :], T.w[:, :]).then_inc(S.sw, 16)
    for q in range(8):
        (g.sync if q % 2 else g.scalar).dma_start(T.idx[16 * q:16 * q + 16, :], T.nb[:, :]).then_inc(S.snb, 16)

    g.wait_ge(S.sx, 16)
    left = 0
    for call in P[rank][1]:
        g.remote_dma_fused([_send(T, topo, core, rank, dsts, m, S[nm]) for dsts, m, nm in call], local_sem=S.sent)
        left += sum(_count(m) for dsts, m, nm in call)

    landed = sum(_count(m) for i in range(N) for h, dst, m, fm in P[i][0] if rank in dst)

    ps = [T.ps0, T.ps1, T.ps2, T.ps3]
    gs = [S.g0, S.g1, S.g2, S.g3]
    ms = [S.m0, S.m1, S.m2, S.m3]
    rs = [S.r0, S.r1, S.r2, S.r3]
    v, s, t = g.vector, g.scalar, g.tensor

    v.wait_ge(S.snb, 128)
    v.tensor_copy(T.off[:, :], T.idx[:, :]).then_inc(S.soff, 1)

    t.wait_ge(S.sx, 16)
    t.wait_ge(S.sw, 16)
    for k in range(NCH):
        t.matmul(ps[k][:, 0:CH], T.wsb[:, :], T.win[:, rank * V + k * CH:rank * V + (k + 1) * CH], True, False)

    for e in (v, s):
        e.wait_ge(S.soff, 1)
        e.wait_ge(S.sx, 16)
        e.wait_ge(S.arr, landed)
    oc = 2 * CH // 16
    for k in range(NCH):
        src = T.win[:, 0:N * V].indirect(T.off[:, k * oc:(k + 1) * oc])
        dst = T.gat[:, k * 2 * CH:(k + 1) * 2 * CH]
        if k % 2 == 0:
            v.tensor_copy(dst, src).then_inc(gs[k], 1)
        else:
            s.activation(dst, src, ActivationFunctionType.Copy).then_inc(gs[k], 1)
    for k in range(NCH):
        t.wait_ge(gs[k], 1)
        t.matmul(ps[k][:, 0:CH], T.wsb[:, :], T.gat[:, k * 2 * CH:(k + 1) * 2 * CH:2], False, False)
        t.matmul(ps[k][:, 0:CH], T.wsb[:, :], T.gat[:, k * 2 * CH + 1:(k + 1) * 2 * CH:2], False, True).then_inc(ms[k], 1)
    for k in range(NCH):
        dst = T.ysb[:, k * CH:(k + 1) * CH]
        if k % 2 == 0:
            v.wait_ge(ms[k], 1)
            v.tensor_scalar(dst, ps[k][:, 0:CH], 0.0, None, AluOpType.max).then_inc(rs[k], 1)
        else:
            s.wait_ge(ms[k], 1)
            s.activation(dst, ps[k][:, 0:CH], ActivationFunctionType.Relu).then_inc(rs[k], 1)
    for a in range(NCH // 2):
        g.sync.wait_ge(rs[2 * a], 1)
        g.sync.wait_ge(rs[2 * a + 1], 1)
        g.sync.dma_start(T.y[:, 2 * a * CH:(2 * a + 2) * CH], T.ysb[:, 2 * a * CH:(2 * a + 2) * CH]).then_inc(S.sy, 16)
    g.sync.wait_ge(S.sy, 16 * (NCH // 2))
    g.wait_ge(S.sent, left)
